import numpy as np
import ml_dtypes


def mxq(x, axis, fmt="e4m3"):
    dtype, down = {"e4m3": (ml_dtypes.float8_e4m3fn, 7), "e5m2": (ml_dtypes.float8_e5m2, 14)}[fmt]
    v = np.moveaxis(np.asarray(x, np.float32).astype(ml_dtypes.bfloat16).astype(np.float64), axis, -1)
    blocks = v.reshape(v.shape[:-1] + (-1, 32))
    amax = np.abs(blocks).max(-1, keepdims=True)
    byte = np.maximum(np.where(amax > 0, np.frexp(amax)[1] - 1 + 127, 0) - down, 1)
    scale = np.exp2(byte - 127.0)
    codes = (blocks / scale).astype(np.float32).astype(dtype).astype(np.float64)
    return np.moveaxis((codes * scale).reshape(v.shape), -1, axis)


WIDE = False


def mx_kscale(k):
    if not WIDE:
        return np.ones(k)
    levels = np.array([10, -10, 5, -5, 0])
    if k % 512:
        return np.exp2(np.random.permutation(np.resize(levels, k // 32))).repeat(32)
    a = np.empty((k // 512, 16))
    for p in range(k // 512):
        a[p, :8] = np.random.permutation(np.resize(levels, 8))
        for g in range(8):
            far = levels[np.abs(levels - a[p, g]) >= 10]
            a[p, g + 8] = far[np.random.randint(len(far))]
    return np.exp2(a.ravel()).repeat(32)


BF16 = ml_dtypes.bfloat16


def bf(x):
    return np.asarray(x, np.float32).astype(BF16)


def f64(x):
    return np.asarray(x).astype(np.float64)


E2M1 = np.array([0.0, 0.5, 1.0, 1.5, 2.0, 3.0, 4.0, 6.0, -0.0, -0.5, -1.0, -1.5, -2.0, -3.0, -4.0, -6.0])


def pack_weight(w, fmt):
    k, n = w.shape
    w = f64(bf(w)).reshape(k // 32, 32, n)
    amax = np.abs(w).max(1)
    if fmt == "e4m3":
        byte = np.frexp(amax)[1] - 1 + 127 - 7
    else:
        mant, ex = np.frexp(amax / 6.0)
        byte = np.where(mant > 0.5, ex, ex - 1) + 127
    byte = np.clip(np.where(amax > 0, byte, 1), 1, 254)
    scaled = (w * np.exp2(127.0 - byte)[:, None, :]).reshape(k, n).astype(np.float32)
    by_word = np.ascontiguousarray(scaled.reshape(k // 512, 128, 4, n).transpose(0, 1, 3, 2))
    if fmt == "e4m3":
        words = by_word.astype(ml_dtypes.float8_e4m3fn).view(np.uint8)
    else:
        c = by_word.astype(ml_dtypes.float4_e2m1fn).view(np.uint8) & 0xF
        words = c[..., 0::2] | (c[..., 1::2] << 4)
    return np.ascontiguousarray(words), np.ascontiguousarray(byte.astype(np.uint8).reshape(k // 512, 16, n))


def unpack_weight(words, scales, fmt):
    g, p, n, _ = words.shape
    if fmt == "e4m3":
        vals = np.ascontiguousarray(words).view(ml_dtypes.float8_e4m3fn).astype(np.float64)
    else:
        nib = np.empty((g, p, n, 4), np.uint8)
        nib[..., 0::2] = words & 0xF
        nib[..., 1::2] = words >> 4
        vals = E2M1[nib]
    vals = vals * np.repeat(np.exp2(scales.astype(np.float64) - 127.0), 8, axis=1)[..., None]
    return vals.transpose(0, 1, 3, 2).reshape(g * 512, n)
def pack4(w):
    words, scales = pack_weight(w, "e2m1")
    return words.reshape(words.shape[0], 128, -1), scales


def unpack4(words, scales):
    return unpack_weight(words.reshape(words.shape[0], 128, -1, 2), scales, "e2m1")


def planes(Y):
    n, m = Y.shape
    b = f64(bf(Y)).reshape(n // 32, 32, m)
    amax = np.abs(b).max(1)
    byte = np.clip(np.where(amax > 0, np.frexp(amax)[1] - 1 + 127 - 7, 1), 1, 254)
    codes = (b * np.exp2(127.0 - byte)[:, None, :]).reshape(n, m).astype(np.float32).astype(ml_dtypes.float8_e4m3fn).view(np.uint8)
    words = codes.reshape(n // 512, 128, 4, m).transpose(0, 1, 3, 2)
    return np.ascontiguousarray(words), np.ascontiguousarray(byte.astype(np.uint8).reshape(n // 512, 16, m))


S, G, H, F = 1024, 1024, 2048, 1536
SPREAD = 0.4
CARRY = 0.5
HALF = 0.5

def setup_inputs():
    sg = mx_kscale(G)
    sh = mx_kscale(H)
    size = np.exp(SPREAD * np.random.randn(F))
    govt_moves = np.random.randn(S, G) * sg[None, :]
    govt_loadings = np.random.randn(G, F) / np.sqrt(G) * size[None, :] / sg[:, None]
    corp_moves = np.random.randn(S, H) * sh[None, :]
    corp_loadings = np.random.randn(H, F) / np.sqrt(H) * size[None, :] / sh[:, None]
    corp_words, corp_scales = pack4(corp_loadings)
    carry = CARRY * np.random.randn(F)
    return {
        "govt_moves": bf(govt_moves),
        "govt_loadings": bf(govt_loadings),
        "corp_moves": bf(corp_moves),
        "corp_words": corp_words,
        "corp_scales": corp_scales,
        "carry": bf(carry),
    }

def reference(govt_moves, govt_loadings, corp_moves, corp_words, corp_scales, carry):
    govt = mxq(f64(govt_moves), 1, "e4m3") @ mxq(f64(govt_loadings), 0, "e4m3")
    corp = mxq(f64(corp_moves), 1, "e4m3") @ unpack4(corp_words, corp_scales)
    move = govt + corp + f64(carry)
    y = HALF * np.square(move)
    Y = y.T
    words, scales = planes(Y)
    return y, words, scales

@@ -1,0 +1,469 @@
+import math
+from contextlib import ExitStack
+
+import concourse.mybir as mybir
+from concourse.masks import make_identity
+
+S, G, H, F = 1024, 1024, 2048, 1536
+FLOPS = 2 * S * (G + H) * F
+
+F32 = mybir.dt.float32
+BF16 = mybir.dt.bfloat16
+I32 = mybir.dt.int32
+U32 = mybir.dt.uint32
+U8 = mybir.dt.uint8
+FP8X4 = mybir.dt.float8_e4m3fn_x4
+FP4X4 = mybir.dt.float4_e2m1fn_x4
+ACT = mybir.ActivationFunctionType
+ALU = mybir.AluOpType
+
+P = 128
+PACK = 4
+KP = P * PACK
+NT = 512
+TILES = S // P
+CHUNKS = F // NT
+A_PASSES = G // KP
+C_PASSES = H // KP
+HALF_TILES = TILES // 2
+ROOT_TWO = math.sqrt(2.0)
+
+
+def tile_half_squared_curve_factors_g5_kernel(
+    tc, govt_moves, govt_loadings, corp_moves, corp_words, corp_scales, carry, out_0, out_1, out_2
+):
+    nc = tc.nc
+    with ExitStack() as ctx:
+        keep = ctx.enter_context(tc.tile_pool(name="keep", bufs=1))
+        work = ctx.enter_context(tc.tile_pool(name="work", bufs=4))
+        psum = ctx.enter_context(tc.psum_pool(name="psum", bufs=1))
+        ctx.enter_context(tc.manual_schedule())
+
+        d_words_hbm = corp_words.bitcast(I32)
+        d_scales_hbm = corp_scales.bitcast(I32)
+        words_hbm = out_1.rearrange("g p m t -> g p (m t)").bitcast(I32)
+        scales_hbm = out_2.bitcast(I32)
+
+        raw = {}
+        banks = {}
+        staged = {}
+        lhs = {}
+        b_ops = {}
+        acc = {}
+        z = {}
+        y = {}
+        y_sorted = {}
+
+        def load_rows(kind, t, split=False):
+            src = corp_moves if kind == "c" else govt_moves
+            width = src.shape[1]
+            step = 2 * KP if split else width
+            for c0 in range(0, width, step):
+                tile = keep.tile([P, step], BF16, name="raw_%s%d_%d" % (kind, t, c0), align_bytes=64)
+                nc.sync.dma_start(out=tile[:], in_=src[t * P : (t + 1) * P, c0 : c0 + step])
+                for c in range(0, step, 2 * KP):
+                    raw[kind, t, (c0 + c) // (2 * KP)] = tile[:, c : c + 2 * KP]
+
+        def load_d(g):
+            raw["d", g] = keep.tile([P, C_PASSES, 2 * NT], U8, name="d_words%d" % g, align_bytes=64)
+            cols = slice(g * NT // 2, (g + 1) * NT // 2)
+            nc.sync.dma_start(
+                out=raw["d", g][:].bitcast(I32), in_=d_words_hbm[:, :, cols].rearrange("k p w -> p k w")
+            )
+
+        def load_b(g, k):
+            raw["b", g, k] = keep.tile([P, PACK, NT], BF16, name="raw_b%d_%d" % (g, k), align_bytes=64)
+            rows = govt_loadings[k * KP : (k + 1) * KP, g * NT : (g + 1) * NT]
+            nc.sync.dma_start(out=raw["b", g, k][:], in_=rows.rearrange("(p t) n -> p t n", t=PACK))
+
+        ident = keep.tile([P, P], F32, name="ident", align_bytes=64)
+        d_scales = keep.tile([P, C_PASSES, F], U8, name="d_scales", align_bytes=64)
+        carry_raw = keep.tile([P, CHUNKS, PACK], BF16, name="carry_raw")
+        carry_col = keep.tile([P, CHUNKS * PACK], BF16, name="carry_col")
+        nc.vector.memset(d_scales[:].rearrange("p k n -> p (k n)").bitcast(I32), 0)
+        nc.gpsimd.dma_start(out=carry_raw[:], in_=carry.rearrange("(g p c) -> p g c", g=CHUNKS, c=PACK))
+        make_identity(nc, ident[:])
+        nc.scalar.activation(out=carry_col[:], in_=carry_raw[:].rearrange("p g c -> p (g c)"), func=ACT.Copy, scale=0.5)
+
+        load_rows("c", 0, split=True)
+        load_d(0)
+        for q in range(4):
+            nc.sync.dma_start(
+                out=d_scales[32 * q : 32 * q + 4, :, :].bitcast(I32),
+                in_=d_scales_hbm[:, 4 * q : 4 * q + 4, :].rearrange("k r w -> r k w"),
+            )
+        load_rows("c", 1)
+        load_rows("c", 2)
+        load_b(0, 0)
+        load_b(0, 1)
+        for t in range(3):
+            load_rows("a", t)
+        load_rows("c", 3)
+        load_rows("a", 3)
+        for g in (1, 2):
+            load_d(g)
+            load_b(g, 0)
+            load_b(g, 1)
+            load_rows("c", 3 + g)
+            load_rows("a", 3 + g)
+        for t in (6, 7):
+            load_rows("c", t)
+            load_rows("a", t)
+
+        def new_bank():
+            bank = psum.tile([P, 4, P], F32, name="turn", tag="turn", bufs=5)
+            return bank
+
+        presorted = {}
+
+        def presort(kind, t, half, on_vector=False):
+            words = raw[kind, t, half].bitcast(F32)
+            presorted[kind, t, half] = work.tile([P, 4, P], F32, name="presorted", tag="presorted", bufs=6, align_bytes=64)
+            dst = presorted[kind, t, half][:].rearrange("s (j u) p -> s j u p", u=2)
+            src = words.rearrange("s (j p u) -> s j u p", j=2, u=2)
+            if on_vector:
+                nc.vector.tensor_copy(out=dst, in_=src)
+            else:
+                nc.scalar.copy(out=dst, in_=src)
+
+        def turn_in(kind, t, half):
+            words = raw[kind, t, half].bitcast(F32)
+            bank = new_bank()
+            banks[kind, t, half] = bank
+            for j in range(2):
+                for u in range(2):
+                    if (kind, t, half) in presorted:
+                        src = presorted[kind, t, half][:, 2 * j + u, :]
+                    else:
+                        src = words[:, 256 * j + u : 256 * (j + 1) : 2]
+                    nc.tensor.transpose(bank[:, 2 * j + u, :], src, ident[:])
+
+        def copy_bank(key, on_vector=False):
+            staged[key] = work.tile([P, 2 * KP], BF16, name="staged", tag="staged", bufs=4, align_bytes=64)
+            dst = staged[key][:].bitcast(F32).rearrange("p (j s u) -> p j s u", j=2, u=2)
+            src = banks[key][:].rearrange("p (j u) s -> p j s u", u=2)
+            if on_vector:
+                nc.vector.tensor_copy(out=dst, in_=src)
+            else:
+                nc.scalar.copy(out=dst, in_=src)
+
+        def quant_in(kind, t, half):
+            codes = keep.tile([P, 2 * P], U32, name="lc_%s%d_%d" % (kind, t, half), align_bytes=64)
+            scales = keep.tile([P, 2 * P], U8, name="ls_%s%d_%d" % (kind, t, half), align_bytes=64)
+            lhs[kind, t, half] = (codes, scales)
+            nc.vector.quantize_mx(out=codes[:].bitcast(FP8X4), scales=scales[:], in_=staged[kind, t, half][:])
+
+        def weave_b(g, k, on_vector, lo=0, hi=NT):
+            if ("b", g, k) not in staged:
+                staged["b", g, k] = work.tile([P, NT * PACK], BF16, name="b_staged", tag="b_staged", bufs=2, align_bytes=64)
+            dst = staged["b", g, k][:, lo * PACK : hi * PACK].rearrange("p (c i t) -> p c t i", i=4, t=PACK)
+            src = raw["b", g, k][:, :, lo:hi].rearrange("p t (c i) -> p c t i", i=4)
+            if on_vector:
+                nc.vector.tensor_copy(out=dst, in_=src)
+            else:
+                nc.scalar.copy(out=dst, in_=src)
+
+        def quant_b(g, k):
+            codes = keep.tile([P, NT], U32, name="bc%d_%d" % (g, k), align_bytes=64)
+            scales = keep.tile([P, NT], U8, name="bs%d_%d" % (g, k), align_bytes=64)
+            b_ops[g, k] = (codes, scales)
+            nc.vector.quantize_mx(out=codes[:].bitcast(FP8X4), scales=scales[:], in_=staged["b", g, k][:])
+
+        carry_row = keep.tile([P, F], BF16, name="carry_row", align_bytes=64)
+
+        def turn_carry(b):
+            words = carry_col[:].bitcast(F32)
+            bank = new_bank()
+            banks["carry", b] = bank
+            for w in range(4 * b, min(4 * b + 4, 2 * CHUNKS)):
+                nc.tensor.transpose(bank[:, w % 4, :], words[:, w : w + 1].to_broadcast([P, P]), ident[:])
+
+        def copy_carry(b):
+            count = min(2, CHUNKS - 2 * b)
+            dst = carry_row[:, 2 * b * NT : (2 * b + count) * NT].bitcast(F32)
+            nc.scalar.copy(
+                out=dst.rearrange("p (j n u) -> p j n u", j=count, u=2),
+                in_=banks["carry", b][:, : 2 * count, :].rearrange("p (j u) n -> p j n u", u=2),
+            )
+
+        def place(u):
+            if u < CHUNKS * HALF_TILES:
+                return u % HALF_TILES, u // HALF_TILES
+            couple, rest = divmod(u - CHUNKS * HALF_TILES, 2 * CHUNKS)
+            return HALF_TILES + 2 * couple + rest % 2, rest // 2
+
+        def mm_c(u):
+            t, g = place(u)
+            acc[u] = psum.tile([P, NT], F32, name="acc", tag="acc", bufs=3)
+            for k in range(C_PASSES):
+                codes, scales = lhs["c", t, k // 2]
+                cols = slice((k % 2) * P, (k % 2 + 1) * P)
+                nc.tensor.matmul_mx(
+                    out=acc[u][:],
+                    lhsT=codes[:, cols].bitcast(FP8X4),
+                    lhsT_scale=scales[:, cols],
+                    rhs=raw["d", g][:, k, :].bitcast(FP4X4),
+                    rhs_scale=d_scales[:, k, g * NT : (g + 1) * NT],
+                    start=(k == 0),
+                    stop=False,
+                )
+
+        def mm_a(u):
+            t, g = place(u)
+            codes, scales = lhs["a", t, 0]
+            for k in range(A_PASSES):
+                cols = slice(k * P, (k + 1) * P)
+                b_codes, b_scales = b_ops[g, k]
+                nc.tensor.matmul_mx(
+                    out=acc[u][:],
+                    lhsT=codes[:, cols].bitcast(FP8X4),
+                    lhsT_scale=scales[:, cols],
+                    rhs=b_codes[:].bitcast(FP8X4),
+                    rhs_scale=b_scales[:],
+                    start=False,
+                    stop=(k == A_PASSES - 1),
+                )
+
+        def add(u):
+            t, g = place(u)
+            z[u] = work.tile([P, NT], F32, name="z", tag="z", bufs=6)
+            nc.vector.scalar_tensor_tensor(
+                out=z[u][:], in0=acc[u][:], scalar=0.5, in1=carry_row[:, g * NT : (g + 1) * NT], op0=ALU.mult, op1=ALU.add
+            )
+
+        def square(u):
+            t, g = place(u)
+            y[u] = work.tile([P, NT], F32, name="y", tag="y", bufs=12)
+            nc.scalar.activation(out=y[u][:], in_=z[u][:], func=ACT.Square, scale=ROOT_TWO)
+            nc.sync.dma_start(out=out_0[t * P : (t + 1) * P, g * NT : (g + 1) * NT], in_=y[u][:])
+
+        def cast(u):
+            y_sorted[u] = work.tile([P, NT], BF16, name="y_sorted", tag="y_sorted", bufs=8, align_bytes=64)
+            nc.vector.tensor_copy(
+                out=y_sorted[u][:].rearrange("s (u p e) -> s u p e", u=2, e=2),
+                in_=y[u][:].rearrange("s (p u e) -> s u p e", u=2, e=2),
+            )
+
+        def turn_out(pair):
+            bank = new_bank()
+            banks["y", pair] = bank
+            for j in range(2):
+                words = y_sorted[2 * pair + j][:].bitcast(F32)
+                for u in range(2):
+                    nc.tensor.transpose(bank[:, 2 * j + u, :], words[:, u * P : (u + 1) * P], ident[:])
+
+        y_scales_0 = keep.tile([P, S], U8, name="y_scales_0", align_bytes=64)
+        y_scales_12 = keep.tile([P, S], U8, name="y_scales_12", align_bytes=64)
+
+        def store_scales(g0, count, cols, queues):
+            plane = y_scales_0 if g0 == 0 else y_scales_12
+            words = slice(cols.start // 4, cols.stop // 4)
+            for q in range(4):
+                queues[q % len(queues)].dma_start(
+                    out=scales_hbm[g0 : g0 + count, 4 * q : 4 * q + 4, words],
+                    in_=plane[32 * q : 32 * q + 4 * count, cols].bitcast(I32),
+                )
+
+        def quant_out(pair):
+            t, g = place(2 * pair)
+            cols = slice(t * P, (t + 2) * P)
+            codes = work.tile([P, 2 * P], U32, name="y_codes", tag="y_codes", bufs=4, align_bytes=64)
+            plane = y_scales_0[:, cols] if g == 0 else y_scales_12[4 * (g - 1) :, cols]
+            nc.vector.quantize_mx(out=codes[:].bitcast(FP8X4), scales=plane, in_=staged["y", pair][:])
+            nc.sync.dma_start(out=words_hbm[g, :, cols], in_=codes[:].bitcast(I32))
+            if pair == 8:
+                store_scales(1, 2, slice(0, 6 * P), [nc.sync])
+            if pair == 9:
+                store_scales(0, 1, slice(0, S), [nc.sync])
+
+        def add_part(u, cols):
+            t, g = place(u)
+            nc.vector.scalar_tensor_tensor(
+                out=z[u][:, cols], in0=acc[u][:, cols], scalar=0.5, in1=carry_row[:, g * NT + cols.start : g * NT + cols.stop], op0=ALU.mult, op1=ALU.add
+            )
+
+        def square_sorted(u, h):
+            nc.scalar.activation(
+                out=y_sorted[u][:].rearrange("s (u p e) -> s u p e", u=2, e=2)[:, :, h * 64 : (h + 1) * 64, :],
+                in_=z[u][:, h * 256 : (h + 1) * 256].rearrange("s (p u e) -> s u p e", u=2, e=2),
+                func=ACT.Square,
+                scale=ROOT_TWO,
+            )
+
+        def turn_one(u):
+            bank = new_bank()
+            banks["one", u] = bank
+            words = y_sorted[u][:].bitcast(F32)
+            for h in range(2):
+                nc.tensor.transpose(bank[:, h, :], words[:, h * P : (h + 1) * P], ident[:])
+
+        def copy_one(u, on_vector):
+            staged["one", u] = work.tile([P, KP], BF16, name="staged_one", tag="staged_one", bufs=2, align_bytes=64)
+            dst = staged["one", u][:].bitcast(F32).rearrange("p (s u) -> p s u", u=2)
+            src = banks["one", u][:, 0:2, :].rearrange("p u s -> p s u")
+            if on_vector:
+                nc.vector.tensor_copy(out=dst, in_=src)
+            else:
+                nc.scalar.copy(out=dst, in_=src)
+
+        def quant_one(u, codes):
+            t, g = place(u)
+            nc.vector.quantize_mx(
+                out=codes[:, (u % 2) * P : (u % 2 + 1) * P].bitcast(FP8X4),
+                scales=y_scales_12[4:, t * P : (t + 1) * P],
+                in_=staged["one", u][:],
+            )
+
+        V, SC = True, False
+        presort("c", 0, 0, V)
+        presort("c", 0, 1, V)
+        turn_in("c", 0, 0)
+        turn_in("c", 0, 1)
+        copy_bank(("c", 0, 0))
+        copy_bank(("c", 0, 1), on_vector=True)
+        turn_carry(0)
+        turn_carry(1)
+        quant_in("c", 0, 0)
+        quant_in("c", 0, 1)
+        mm_c(0)
+        presort("c", 1, 0, SC)
+        presort("c", 1, 1, V)
+        presort("c", 2, 0, V)
+        presort("c", 2, 1, V)
+        copy_carry(0)
+        copy_carry(1)
+        for t in (1, 2):
+            for half in range(2):
+                turn_in("c", t, half)
+                copy_bank(("c", t, half))
+        weave_b(0, 0, V)
+        quant_in("c", 1, 0)
+        quant_in("c", 1, 1)
+        mm_c(1)
+        presort("a", 0, 0, V)
+        presort("a", 1, 0, SC)
+        quant_b(0, 0)
+        quant_in("c", 2, 0)
+        quant_in("c", 2, 1)
+        weave_b(0, 1, V)
+        for t in (0, 1):
+            turn_in("a", t, 0)
+            copy_bank(("a", t, 0))
+        mm_c(2)
+        quant_in("a", 0, 0)
+        quant_b(0, 1)
+        presort("a", 2, 0, SC)
+        presort("c", 3, 0, SC)
+        quant_in("a", 1, 0)
+        presort("c", 3, 1, V)
+        presort("a", 3, 0, V)
+        for key in (("a", 2, 0), ("c", 3, 0), ("c", 3, 1), ("a", 3, 0)):
+            turn_in(*key)
+            copy_bank(key)
+        mm_a(0)
+        quant_in("a", 2, 0)
+        add(0)
+        mm_a(1)
+        for key in (("c", 3, 0), ("c", 3, 1), ("a", 3, 0)):
+            quant_in(*key)
+        mm_a(2)
+        weave_b(1, 0, SC)
+        add(1)
+        weave_b(1, 1, V)
+        mm_c(3)
+        mm_a(3)
+        mm_c(4)
+        add(2)
+        quant_b(1, 1)
+        quant_b(1, 0)
+        mm_c(5)
+        mm_a(4)
+        square(0)
+        square(1)
+        add(3)
+        mm_a(5)
+        square(2)
+        cast(0)
+        cast(1)
+        add(4)
+        square(3)
+        cast(2)
+        weave_b(2, 0, V)
+        cast(3)
+        quant_b(2, 0)
+        square(4)
+
+        def tile_keys(pair):
+            t = {4: 4, 5: 5, 7: 6, 8: 7}.get(pair)
+            return [] if t is None else [("c", t, 0), ("c", t, 1), ("a", t, 0)]
+
+        for pair in range(3, 11):
+            keys = tile_keys(pair)
+            ahead = tile_keys(pair + 1)
+            outs = {3: [0], 4: [1], 5: [2], 6: [3, 4], 9: [], 10: [7, 8]}.get(pair, [pair - 2])
+            for o in outs:
+                turn_out(o)
+            for key in keys:
+                turn_in(*key)
+            add(2 * pair - 1)
+            cast(2 * pair - 2)
+            for o in outs[:1]:
+                copy_bank(("y", o))
+            square(2 * pair - 1)
+            for o in outs[1:]:
+                copy_bank(("y", o))
+            for o in outs[:1]:
+                quant_out(o)
+            cast(2 * pair - 1)
+            for o in outs[1:]:
+                quant_out(o)
+            for key in ahead[2:]:
+                presort(*key, on_vector=True)
+            for key in keys:
+                copy_bank(key)
+                quant_in(*key)
+            for key in ahead[:2]:
+                presort(*key)
+            mm_c(2 * pair)
+            mm_a(2 * pair)
+            if pair == 3:
+                weave_b(2, 1, V)
+            add(2 * pair)
+            square(2 * pair)
+            if pair == 3:
+                quant_b(2, 1)
+            mm_c(2 * pair + 1)
+            mm_a(2 * pair + 1)
+
+        add(21)
+        cast(20)
+        square(21)
+        mm_c(22)
+        mm_a(22)
+        cast(21)
+        turn_out(9)
+        turn_out(10)
+        mm_c(23)
+        mm_a(23)
+        add(22)
+        copy_bank(("y", 9))
+        square(22)
+        quant_out(9)
+        copy_bank(("y", 10))
+        cast(22)
+        turn_one(22)
+        z[23] = work.tile([P, NT], F32, name="z", tag="z", bufs=6)
+        y_sorted[23] = work.tile([P, NT], BF16, name="y_sorted", tag="y_sorted", bufs=8, align_bytes=64)
+        codes = work.tile([P, 2 * P], U32, name="y_codes", tag="y_codes", bufs=4, align_bytes=64)
+        for h in range(2):
+            add_part(23, slice(h * 256, (h + 1) * 256))
+            square_sorted(23, h)
+        quant_out(10)
+        turn_one(23)
+        copy_one(22, V)
+        square(23)
+        quant_one(22, codes)
+        copy_one(23, V)
+        quant_one(23, codes)
+        nc.sync.dma_start(out=words_hbm[2, :, 6 * P : 8 * P], in_=codes[:].bitcast(I32))
+        store_scales(1, 2, slice(6 * P, S), [nc.scalar, nc.sync])

@@ -139,7 +139,7 @@ def tile_half_squared_curve_factors_g5_kernel(
                     nc.tensor.transpose(bank[:, 2 * j + u, :], src, ident[:])
 
         def copy_bank(key, on_vector=False):
-            staged[key] = work.tile([P, 2 * KP], BF16, name="staged", tag="staged", bufs=4, align_bytes=64)
+            staged[key] = work.tile([P, 2 * KP], BF16, name="staged", tag="staged", bufs=5, align_bytes=64)
             dst = staged[key][:].bitcast(F32).rearrange("p (j s u) -> p j s u", j=2, u=2)
             src = banks[key][:].rearrange("p (j u) s -> p j s u", u=2)
             if on_vector:
@@ -238,7 +238,7 @@ def tile_half_squared_curve_factors_g5_kernel(
             nc.sync.dma_start(out=out_0[t * P : (t + 1) * P, g * NT : (g + 1) * NT], in_=y[u][:])
 
         def cast(u):
-            y_sorted[u] = work.tile([P, NT], BF16, name="y_sorted", tag="y_sorted", bufs=8, align_bytes=64)
+            y_sorted[u] = work.tile([P, NT], BF16, name="y_sorted", tag="y_sorted", bufs=10, align_bytes=64)
             nc.vector.tensor_copy(
                 out=y_sorted[u][:].rearrange("s (u p e) -> s u p e", u=2, e=2),
                 in_=y[u][:].rearrange("s (p u e) -> s u p e", u=2, e=2),
@@ -252,29 +252,32 @@ def tile_half_squared_curve_factors_g5_kernel(
                 for u in range(2):
                     nc.tensor.transpose(bank[:, 2 * j + u, :], words[:, u * P : (u + 1) * P], ident[:])
 
-        y_scales_0 = keep.tile([P, S], U8, name="y_scales_0", align_bytes=64)
-        y_scales_12 = keep.tile([P, S], U8, name="y_scales_12", align_bytes=64)
+        early = 6 * P
+        y_scales = [
+            keep.tile([P, CHUNKS, early], U8, name="y_scales_early", align_bytes=64),
+            keep.tile([P, CHUNKS, S - early], U8, name="y_scales_late", align_bytes=64),
+        ]
 
-        def store_scales(g0, count, cols, queues):
-            plane = y_scales_0 if g0 == 0 else y_scales_12
-            words = slice(cols.start // 4, cols.stop // 4)
+        def plane_of(g, m0, width):
+            if m0 < early:
+                return y_scales[0][:, g, m0 : m0 + width]
+            return y_scales[1][:, g, m0 - early : m0 - early + width]
+
+        def store_scales(part, queues):
+            words = slice(0, early // 4) if part == 0 else slice(early // 4, S // 4)
             for q in range(4):
                 queues[q % len(queues)].dma_start(
-                    out=scales_hbm[g0 : g0 + count, 4 * q : 4 * q + 4, words],
-                    in_=plane[32 * q : 32 * q + 4 * count, cols].bitcast(I32),
+                    out=scales_hbm[:, 4 * q : 4 * q + 4, words].rearrange("g r w -> r g w"),
+                    in_=y_scales[part][32 * q : 32 * q + 4, :, :].bitcast(I32),
                 )
 
         def quant_out(pair):
             t, g = place(2 * pair)
-            cols = slice(t * P, (t + 2) * P)
             codes = work.tile([P, 2 * P], U32, name="y_codes", tag="y_codes", bufs=4, align_bytes=64)
-            plane = y_scales_0[:, cols] if g == 0 else y_scales_12[4 * (g - 1) :, cols]
-            nc.vector.quantize_mx(out=codes[:].bitcast(FP8X4), scales=plane, in_=staged["y", pair][:])
-            nc.sync.dma_start(out=words_hbm[g, :, cols], in_=codes[:].bitcast(I32))
+            nc.vector.quantize_mx(out=codes[:].bitcast(FP8X4), scales=plane_of(g, t * P, 2 * P), in_=staged["y", pair][:])
+            nc.sync.dma_start(out=words_hbm[g, :, t * P : (t + 2) * P], in_=codes[:].bitcast(I32))
             if pair == 8:
-                store_scales(1, 2, slice(0, 6 * P), [nc.sync])
-            if pair == 9:
-                store_scales(0, 1, slice(0, S), [nc.sync])
+                store_scales(0, [nc.sync])
 
         def add_part(u, cols):
             t, g = place(u)
@@ -310,14 +313,13 @@ def tile_half_squared_curve_factors_g5_kernel(
             t, g = place(u)
             nc.vector.quantize_mx(
                 out=codes[:, (u % 2) * P : (u % 2 + 1) * P].bitcast(FP8X4),
-                scales=y_scales_12[4:, t * P : (t + 1) * P],
+                scales=plane_of(g, t * P, P),
                 in_=staged["one", u][:],
             )
 
         V, SC = True, False
-        presort("c", 0, 0, V)
-        presort("c", 0, 1, V)
         turn_in("c", 0, 0)
+        presort("c", 0, 1, V)
         turn_in("c", 0, 1)
         copy_bank(("c", 0, 0))
         copy_bank(("c", 0, 1), on_vector=True)
@@ -325,145 +327,139 @@ def tile_half_squared_curve_factors_g5_kernel(
         turn_carry(1)
         quant_in("c", 0, 0)
         quant_in("c", 0, 1)
+        turn_in("c", 1, 0)
+        turn_in("c", 1, 1)
         mm_c(0)
-        presort("c", 1, 0, SC)
-        presort("c", 1, 1, V)
         presort("c", 2, 0, V)
         presort("c", 2, 1, V)
         copy_carry(0)
+        copy_bank(("c", 1, 0))
+        copy_bank(("c", 1, 1))
         copy_carry(1)
-        for t in (1, 2):
-            for half in range(2):
-                turn_in("c", t, half)
-                copy_bank(("c", t, half))
-        weave_b(0, 0, V)
+        turn_in("c", 2, 0)
+        turn_in("c", 2, 1)
         quant_in("c", 1, 0)
         quant_in("c", 1, 1)
         mm_c(1)
-        presort("a", 0, 0, V)
-        presort("a", 1, 0, SC)
-        quant_b(0, 0)
+        weave_b(0, 0, V)
+        copy_bank(("c", 2, 0))
+        copy_bank(("c", 2, 1))
+        weave_b(0, 1, V)
         quant_in("c", 2, 0)
         quant_in("c", 2, 1)
-        weave_b(0, 1, V)
-        for t in (0, 1):
+        quant_b(0, 0)
+        quant_b(0, 1)
+        for t in (0, 1, 2):
             turn_in("a", t, 0)
+        for t in (0, 1, 2):
             copy_bank(("a", t, 0))
         mm_c(2)
-        quant_in("a", 0, 0)
-        quant_b(0, 1)
-        presort("a", 2, 0, SC)
-        presort("c", 3, 0, SC)
-        quant_in("a", 1, 0)
+        presort("c", 3, 0, V)
         presort("c", 3, 1, V)
+        quant_in("a", 0, 0)
         presort("a", 3, 0, V)
-        for key in (("a", 2, 0), ("c", 3, 0), ("c", 3, 1), ("a", 3, 0)):
+        for t in (1, 2):
+            quant_in("a", t, 0)
+        third = (("c", 3, 0), ("c", 3, 1), ("a", 3, 0))
+        for key in third:
             turn_in(*key)
             copy_bank(key)
         mm_a(0)
-        quant_in("a", 2, 0)
-        add(0)
         mm_a(1)
-        for key in (("c", 3, 0), ("c", 3, 1), ("a", 3, 0)):
-            quant_in(*key)
         mm_a(2)
-        weave_b(1, 0, SC)
+        weave_b(1, 0, V, 0, 256)
+        quant_in(*third[0])
+        add(0)
+        quant_in(*third[1])
+        weave_b(1, 0, SC, 256, 512)
+        quant_in(*third[2])
         add(1)
-        weave_b(1, 1, V)
+        weave_b(1, 1, SC, 256, 512)
+        weave_b(1, 1, V, 0, 256)
         mm_c(3)
         mm_a(3)
         mm_c(4)
         add(2)
-        quant_b(1, 1)
         quant_b(1, 0)
+        quant_b(1, 1)
         mm_c(5)
         mm_a(4)
+        mm_a(5)
         square(0)
         square(1)
         add(3)
-        mm_a(5)
         square(2)
         cast(0)
+        presort("c", 4, 0, V)
         cast(1)
-        add(4)
+        presort("c", 4, 1, V)
         square(3)
+        add(4)
         cast(2)
-        weave_b(2, 0, V)
-        cast(3)
-        quant_b(2, 0)
-        square(4)
 
-        def tile_keys(pair):
-            t = {4: 4, 5: 5, 7: 6, 8: 7}.get(pair)
-            return [] if t is None else [("c", t, 0), ("c", t, 1), ("a", t, 0)]
-
-        for pair in range(3, 11):
-            keys = tile_keys(pair)
-            ahead = tile_keys(pair + 1)
-            outs = {3: [0], 4: [1], 5: [2], 6: [3, 4], 9: [], 10: [7, 8]}.get(pair, [pair - 2])
-            for o in outs:
-                turn_out(o)
+        later = [(kind, t, half) for t in range(HALF_TILES, TILES) for kind, half in (("c", 0), ("c", 1), ("a", 0))]
+        for pair in range(3, 12):
+            keys = later[2 * (pair - 3) : 2 * (pair - 2)]
+            ahead = later[2 * (pair - 2) : 2 * (pair - 1)]
+            outs = [pair - 3] if pair < 9 else []
             for key in keys:
                 turn_in(*key)
+            for o in outs:
+                turn_out(o)
+            square(2 * pair - 2)
+            cast(2 * pair - 3)
             add(2 * pair - 1)
-            cast(2 * pair - 2)
-            for o in outs[:1]:
-                copy_bank(("y", o))
-            square(2 * pair - 1)
-            for o in outs[1:]:
-                copy_bank(("y", o))
-            for o in outs[:1]:
-                quant_out(o)
-            cast(2 * pair - 1)
-            for o in outs[1:]:
-                quant_out(o)
-            for key in ahead[2:]:
-                presort(*key, on_vector=True)
+            for key in ahead[:1]:
+                presort(*key, on_vector=False)
             for key in keys:
                 copy_bank(key)
+            for o in outs:
+                copy_bank(("y", o))
+            cast(2 * pair - 2)
+            for key in ahead[1:]:
+                presort(*key, on_vector=True)
+            if pair == 3:
+                weave_b(2, 0, V)
+                weave_b(2, 1, SC)
+            square(2 * pair - 1)
+            for key in keys:
                 quant_in(*key)
-            for key in ahead[:2]:
-                presort(*key)
             mm_c(2 * pair)
             mm_a(2 * pair)
             if pair == 3:
-                weave_b(2, 1, V)
+                quant_b(2, 0)
+            late = {10: [6, 7, 8], 11: [9]}.get(pair, [])
+            for o in late:
+                turn_out(o)
             add(2 * pair)
-            square(2 * pair)
+            for o in late:
+                copy_bank(("y", o))
+            if pair == 11:
+                cast(21)
+                square(22)
+            for o in outs + late:
+                quant_out(o)
             if pair == 3:
                 quant_b(2, 1)
             mm_c(2 * pair + 1)
             mm_a(2 * pair + 1)
 
-        add(21)
-        cast(20)
-        square(21)
-        mm_c(22)
-        mm_a(22)
-        cast(21)
-        turn_out(9)
-        turn_out(10)
-        mm_c(23)
-        mm_a(23)
-        add(22)
-        copy_bank(("y", 9))
-        square(22)
-        quant_out(9)
-        copy_bank(("y", 10))
         cast(22)
+        turn_out(10)
         turn_one(22)
         z[23] = work.tile([P, NT], F32, name="z", tag="z", bufs=6)
-        y_sorted[23] = work.tile([P, NT], BF16, name="y_sorted", tag="y_sorted", bufs=8, align_bytes=64)
-        codes = work.tile([P, 2 * P], U32, name="y_codes", tag="y_codes", bufs=4, align_bytes=64)
+        y_sorted[23] = work.tile([P, NT], BF16, name="y_sorted", tag="y_sorted", bufs=10, align_bytes=64)
         for h in range(2):
             add_part(23, slice(h * 256, (h + 1) * 256))
             square_sorted(23, h)
-        quant_out(10)
         turn_one(23)
-        copy_one(22, V)
         square(23)
+        copy_bank(("y", 10), V)
+        copy_one(22, V)
+        quant_out(10)
+        codes = work.tile([P, 2 * P], U32, name="y_codes", tag="y_codes", bufs=4, align_bytes=64)
         quant_one(22, codes)
         copy_one(23, V)
         quant_one(23, codes)
         nc.sync.dma_start(out=words_hbm[2, :, 6 * P : 8 * P], in_=codes[:].bitcast(I32))
-        store_scales(1, 2, slice(6 * P, S), [nc.scalar, nc.sync])
+        store_scales(1, [nc.scalar, nc.sync])

@@ -19,203 +19,198 @@ ALU = mybir.AluOpType
 
 P = 128
 PACK = 4
-KP = P * PACK
-NT = 512
+K_PASS = P * PACK
+STRIP = 2 * K_PASS
+CHUNK = 512
 TILES = S // P
-CHUNKS = F // NT
-A_PASSES = G // KP
-C_PASSES = H // KP
-HALF_TILES = TILES // 2
+CHUNKS = F // CHUNK
+A_PASSES = G // K_PASS
+C_PASSES = H // K_PASS
+UNITS = TILES * CHUNKS
+PAIRS = UNITS // 2
+FIRST = 4
+EARLY = S - 2 * P
+VECTOR_COLUMNS = (384, 192, 256)
+TURN_LAG = 4
 ROOT_TWO = math.sqrt(2.0)
+
+
+def place(unit):
+    if unit < CHUNKS * FIRST:
+        return unit % FIRST, unit // FIRST
+    couple, rest = divmod(unit - CHUNKS * FIRST, 2 * CHUNKS)
+    return FIRST + 2 * couple + rest % 2, rest // 2
 
 
 def tile_half_squared_curve_factors_g5_kernel(
     tc, govt_moves, govt_loadings, corp_moves, corp_words, corp_scales, carry, out_0, out_1, out_2
 ):
     nc = tc.nc
+    on_vector = nc.vector.tensor_copy
+    on_scalar = nc.scalar.copy
     with ExitStack() as ctx:
         keep = ctx.enter_context(tc.tile_pool(name="keep", bufs=1))
         work = ctx.enter_context(tc.tile_pool(name="work", bufs=4))
-        psum = ctx.enter_context(tc.psum_pool(name="psum", bufs=1))
+        psum = ctx.enter_context(tc.psum_pool(name="psum", bufs=4))
         ctx.enter_context(tc.manual_schedule())
 
         d_words_hbm = corp_words.bitcast(I32)
         d_scales_hbm = corp_scales.bitcast(I32)
-        words_hbm = out_1.rearrange("g p m t -> g p (m t)").bitcast(I32)
-        scales_hbm = out_2.bitcast(I32)
+        y_words_hbm = out_1.rearrange("g p m t -> g p (m t)").bitcast(I32)
+        y_scales_hbm = out_2.bitcast(I32)
 
-        raw = {}
-        banks = {}
-        staged = {}
-        lhs = {}
-        b_ops = {}
-        acc = {}
-        z = {}
-        y = {}
-        y_sorted = {}
-
-        def load_rows(kind, t, split=False):
-            src = corp_moves if kind == "c" else govt_moves
-            width = src.shape[1]
-            step = 2 * KP if split else width
-            for c0 in range(0, width, step):
-                tile = keep.tile([P, step], BF16, name="raw_%s%d_%d" % (kind, t, c0), align_bytes=64)
-                nc.sync.dma_start(out=tile[:], in_=src[t * P : (t + 1) * P, c0 : c0 + step])
-                for c in range(0, step, 2 * KP):
-                    raw[kind, t, (c0 + c) // (2 * KP)] = tile[:, c : c + 2 * KP]
-
-        def load_d(g):
-            raw["d", g] = keep.tile([P, C_PASSES, 2 * NT], U8, name="d_words%d" % g, align_bytes=64)
-            cols = slice(g * NT // 2, (g + 1) * NT // 2)
-            nc.sync.dma_start(
-                out=raw["d", g][:].bitcast(I32), in_=d_words_hbm[:, :, cols].rearrange("k p w -> p k w")
-            )
-
-        def load_b(g, k):
-            raw["b", g, k] = keep.tile([P, PACK, NT], BF16, name="raw_b%d_%d" % (g, k), align_bytes=64)
-            rows = govt_loadings[k * KP : (k + 1) * KP, g * NT : (g + 1) * NT]
-            nc.sync.dma_start(out=raw["b", g, k][:], in_=rows.rearrange("(p t) n -> p t n", t=PACK))
+        strips, sorted_strips, banks, staged, lhs = {}, {}, {}, {}, {}
+        d_words, b_rows, b_staged, b_mx = {}, {}, {}, {}
+        acc, z, y, y_sorted, y_codes = {}, {}, {}, {}, {}
 
         ident = keep.tile([P, P], F32, name="ident", align_bytes=64)
-        d_scales = keep.tile([P, C_PASSES, F], U8, name="d_scales", align_bytes=64)
+        d_scales = [keep.tile([P, C_PASSES, CHUNK], U8, name="d_scales%d" % g, align_bytes=64) for g in range(CHUNKS)]
         carry_raw = keep.tile([P, CHUNKS, PACK], BF16, name="carry_raw")
-        carry_col = keep.tile([P, CHUNKS * PACK], BF16, name="carry_col")
-        nc.vector.memset(d_scales[:].rearrange("p k n -> p (k n)").bitcast(I32), 0)
+        carry_half = keep.tile([P, CHUNKS * PACK], BF16, name="carry_half")
+        for g in range(CHUNKS):
+            nc.vector.memset(d_scales[g][:].rearrange("p k n -> p (k n)").bitcast(I32), 0)
         nc.gpsimd.dma_start(out=carry_raw[:], in_=carry.rearrange("(g p c) -> p g c", g=CHUNKS, c=PACK))
         make_identity(nc, ident[:])
-        nc.scalar.activation(out=carry_col[:], in_=carry_raw[:].rearrange("p g c -> p (g c)"), func=ACT.Copy, scale=0.5)
+        nc.scalar.activation(
+            out=carry_half[:], in_=carry_raw[:].rearrange("p g c -> p (g c)"), func=ACT.Copy, scale=0.5
+        )
 
-        load_rows("c", 0, split=True)
-        load_d(0)
-        for q in range(4):
+        def load_rows(kind, t, width):
+            src = corp_moves if kind == "c" else govt_moves
+            for k0 in range(0, src.shape[1], width):
+                rows = keep.tile([P, width], BF16, name="rows_%s%d_%d" % (kind, t, k0), align_bytes=64)
+                nc.sync.dma_start(out=rows[:], in_=src[t * P : (t + 1) * P, k0 : k0 + width])
+                for k in range(0, width, STRIP):
+                    strips[kind, t, (k0 + k) // STRIP] = rows[:, k : k + STRIP]
+
+        def load_d_words(g):
+            d_words[g] = keep.tile([P, C_PASSES, 2 * CHUNK], U8, name="d_words%d" % g, align_bytes=64)
+            cols = slice(g * CHUNK // 2, (g + 1) * CHUNK // 2)
             nc.sync.dma_start(
-                out=d_scales[32 * q : 32 * q + 4, :, :].bitcast(I32),
-                in_=d_scales_hbm[:, 4 * q : 4 * q + 4, :].rearrange("k r w -> r k w"),
+                out=d_words[g][:].bitcast(I32), in_=d_words_hbm[:, :, cols].rearrange("k p w -> p k w")
             )
-        load_rows("c", 1)
-        load_rows("c", 2)
-        load_b(0, 0)
-        load_b(0, 1)
-        for t in range(3):
-            load_rows("a", t)
-        load_rows("c", 3)
-        load_rows("a", 3)
-        for g in (1, 2):
-            load_d(g)
-            load_b(g, 0)
-            load_b(g, 1)
-            load_rows("c", 3 + g)
-            load_rows("a", 3 + g)
-        for t in (6, 7):
-            load_rows("c", t)
-            load_rows("a", t)
 
-        def new_bank():
-            bank = psum.tile([P, 4, P], F32, name="turn", tag="turn", bufs=5)
-            return bank
+        def load_d_scales(g):
+            cols = slice(g * CHUNK // 4, (g + 1) * CHUNK // 4)
+            for q in range(4):
+                nc.sync.dma_start(
+                    out=d_scales[g][32 * q : 32 * q + 4, :, :].bitcast(I32),
+                    in_=d_scales_hbm[:, 4 * q : 4 * q + 4, cols].rearrange("k r w -> r k w"),
+                )
 
-        presorted = {}
+        def load_b(g, k):
+            b_rows[g, k] = keep.tile([P, PACK, CHUNK], BF16, name="b_rows%d_%d" % (g, k), align_bytes=64)
+            rows = govt_loadings[k * K_PASS : (k + 1) * K_PASS, g * CHUNK : (g + 1) * CHUNK]
+            nc.sync.dma_start(out=b_rows[g, k][:], in_=rows.rearrange("(p t) n -> p t n", t=PACK))
 
-        def presort(kind, t, half, on_vector=False):
-            words = raw[kind, t, half].bitcast(F32)
-            presorted[kind, t, half] = work.tile([P, 4, P], F32, name="presorted", tag="presorted", bufs=6, align_bytes=64)
-            dst = presorted[kind, t, half][:].rearrange("s (j u) p -> s j u p", u=2)
-            src = words.rearrange("s (j p u) -> s j u p", j=2, u=2)
-            if on_vector:
-                nc.vector.tensor_copy(out=dst, in_=src)
+        load_rows("c", 0, STRIP)
+        load_rows("c", 1, H)
+        load_d_scales(0)
+        load_d_words(0)
+        for t in range(2, FIRST):
+            load_rows("c", t, H)
+        for k in range(A_PASSES):
+            load_b(0, k)
+            load_rows("a", 2 * k, G)
+            load_rows("a", 2 * k + 1, G)
+        load_d_words(1)
+        load_d_scales(1)
+        load_b(1, 0)
+        load_b(1, 1)
+        load_d_words(2)
+        load_b(2, 0)
+        load_rows("c", FIRST, H)
+        load_b(2, 1)
+        load_d_scales(2)
+        load_rows("a", FIRST, G)
+        for t in range(FIRST + 1, TILES):
+            load_rows("c", t, H)
+            load_rows("a", t, G)
+
+        def sort_strip(key, copy):
+            sorted_strips[key] = work.tile([P, 4, P], F32, name="sorted_strip", bufs=6, align_bytes=64)
+            copy(
+                out=sorted_strips[key][:].rearrange("s (j u) p -> s j u p", u=2),
+                in_=strips[key].bitcast(F32).rearrange("s (j p u) -> s j u p", j=2, u=2),
+            )
+
+        def turn(key, sources):
+            banks[key] = psum.tile([P, 4, P], F32, name="turned")
+            for slot, source in enumerate(sources):
+                nc.tensor.transpose(banks[key][:, slot, :], source, ident[:])
+
+        def turn_strip(key):
+            if key in sorted_strips:
+                turn(key, [sorted_strips[key][:, slot, :] for slot in range(4)])
             else:
-                nc.scalar.copy(out=dst, in_=src)
+                duos = strips[key].bitcast(F32)
+                turn(key, [duos[:, 2 * P * j + u : 2 * P * (j + 1) : 2] for j in range(2) for u in range(2)])
 
-        def turn_in(kind, t, half):
-            words = raw[kind, t, half].bitcast(F32)
-            bank = new_bank()
-            banks[kind, t, half] = bank
-            for j in range(2):
-                for u in range(2):
-                    if (kind, t, half) in presorted:
-                        src = presorted[kind, t, half][:, 2 * j + u, :]
-                    else:
-                        src = words[:, 256 * j + u : 256 * (j + 1) : 2]
-                    nc.tensor.transpose(bank[:, 2 * j + u, :], src, ident[:])
+        def interleave(key, dst, count, copy):
+            copy(
+                out=dst.bitcast(F32).rearrange("p (j s u) -> p j s u", j=count, u=2),
+                in_=banks[key][:, : 2 * count, :].rearrange("p (j u) s -> p j s u", u=2),
+            )
 
-        def copy_bank(key, on_vector=False):
-            staged[key] = work.tile([P, 2 * KP], BF16, name="staged", tag="staged", bufs=5, align_bytes=64)
-            dst = staged[key][:].bitcast(F32).rearrange("p (j s u) -> p j s u", j=2, u=2)
-            src = banks[key][:].rearrange("p (j u) s -> p j s u", u=2)
-            if on_vector:
-                nc.vector.tensor_copy(out=dst, in_=src)
-            else:
-                nc.scalar.copy(out=dst, in_=src)
+        def stage(key, copy):
+            staged[key] = work.tile([P, STRIP], BF16, name="staged", bufs=5, align_bytes=64)
+            interleave(key, staged[key][:], 2, copy)
 
-        def quant_in(kind, t, half):
-            codes = keep.tile([P, 2 * P], U32, name="lc_%s%d_%d" % (kind, t, half), align_bytes=64)
-            scales = keep.tile([P, 2 * P], U8, name="ls_%s%d_%d" % (kind, t, half), align_bytes=64)
-            lhs[kind, t, half] = (codes, scales)
-            nc.vector.quantize_mx(out=codes[:].bitcast(FP8X4), scales=scales[:], in_=staged[kind, t, half][:])
+        def quantise_strip(key):
+            codes = keep.tile([P, 2 * P], U32, name="lhs_codes_%s%d_%d" % key, align_bytes=64)
+            scales = keep.tile([P, 2 * P], U8, name="lhs_scales_%s%d_%d" % key, align_bytes=64)
+            lhs[key] = (codes, scales)
+            nc.vector.quantize_mx(out=codes[:].bitcast(FP8X4), scales=scales[:], in_=staged[key][:])
 
-        def weave_b(g, k, on_vector, lo=0, hi=NT):
-            if ("b", g, k) not in staged:
-                staged["b", g, k] = work.tile([P, NT * PACK], BF16, name="b_staged", tag="b_staged", bufs=2, align_bytes=64)
-            dst = staged["b", g, k][:, lo * PACK : hi * PACK].rearrange("p (c i t) -> p c t i", i=4, t=PACK)
-            src = raw["b", g, k][:, :, lo:hi].rearrange("p t (c i) -> p c t i", i=4)
-            if on_vector:
-                nc.vector.tensor_copy(out=dst, in_=src)
-            else:
-                nc.scalar.copy(out=dst, in_=src)
+        def weave_b(g, k, copy):
+            if (g, k) not in b_staged:
+                b_staged[g, k] = work.tile([P, CHUNK * PACK], BF16, name="b_staged", bufs=2, align_bytes=64)
+            lo, hi = (0, VECTOR_COLUMNS[g]) if copy == on_vector else (VECTOR_COLUMNS[g], CHUNK)
+            copy(
+                out=b_staged[g, k][:, lo * PACK : hi * PACK].rearrange("p (c i t) -> p c t i", i=4, t=PACK),
+                in_=b_rows[g, k][:, :, lo:hi].rearrange("p t (c i) -> p c t i", i=4),
+            )
 
-        def quant_b(g, k):
-            codes = keep.tile([P, NT], U32, name="bc%d_%d" % (g, k), align_bytes=64)
-            scales = keep.tile([P, NT], U8, name="bs%d_%d" % (g, k), align_bytes=64)
-            b_ops[g, k] = (codes, scales)
-            nc.vector.quantize_mx(out=codes[:].bitcast(FP8X4), scales=scales[:], in_=staged["b", g, k][:])
+        def quantise_b(g, k):
+            codes = keep.tile([P, CHUNK], U32, name="b_codes%d_%d" % (g, k), align_bytes=64)
+            scales = keep.tile([P, CHUNK], U8, name="b_scales%d_%d" % (g, k), align_bytes=64)
+            b_mx[g, k] = (codes, scales)
+            nc.vector.quantize_mx(out=codes[:].bitcast(FP8X4), scales=scales[:], in_=b_staged[g, k][:])
 
         carry_row = keep.tile([P, F], BF16, name="carry_row", align_bytes=64)
 
-        def turn_carry(b):
-            words = carry_col[:].bitcast(F32)
-            bank = new_bank()
-            banks["carry", b] = bank
-            for w in range(4 * b, min(4 * b + 4, 2 * CHUNKS)):
-                nc.tensor.transpose(bank[:, w % 4, :], words[:, w : w + 1].to_broadcast([P, P]), ident[:])
+        def turn_carry(g0, count):
+            duos = carry_half[:].bitcast(F32)
+            columns = range(2 * g0, 2 * (g0 + count))
+            turn(("carry", g0), [duos[:, w : w + 1].to_broadcast([P, P]) for w in columns])
 
-        def copy_carry(b):
-            count = min(2, CHUNKS - 2 * b)
-            dst = carry_row[:, 2 * b * NT : (2 * b + count) * NT].bitcast(F32)
-            nc.scalar.copy(
-                out=dst.rearrange("p (j n u) -> p j n u", j=count, u=2),
-                in_=banks["carry", b][:, : 2 * count, :].rearrange("p (j u) n -> p j n u", u=2),
-            )
+        def stage_carry(g0, count):
+            interleave(("carry", g0), carry_row[:, g0 * CHUNK : (g0 + count) * CHUNK], count, on_scalar)
 
-        def place(u):
-            if u < CHUNKS * HALF_TILES:
-                return u % HALF_TILES, u // HALF_TILES
-            couple, rest = divmod(u - CHUNKS * HALF_TILES, 2 * CHUNKS)
-            return HALF_TILES + 2 * couple + rest % 2, rest // 2
-
-        def mm_c(u):
-            t, g = place(u)
-            acc[u] = psum.tile([P, NT], F32, name="acc", tag="acc", bufs=3)
+        def matmul_c(unit):
+            t, g = place(unit)
+            acc[unit] = psum.tile([P, CHUNK], F32, name="acc")
             for k in range(C_PASSES):
                 codes, scales = lhs["c", t, k // 2]
                 cols = slice((k % 2) * P, (k % 2 + 1) * P)
                 nc.tensor.matmul_mx(
-                    out=acc[u][:],
+                    out=acc[unit][:],
                     lhsT=codes[:, cols].bitcast(FP8X4),
                     lhsT_scale=scales[:, cols],
-                    rhs=raw["d", g][:, k, :].bitcast(FP4X4),
-                    rhs_scale=d_scales[:, k, g * NT : (g + 1) * NT],
+                    rhs=d_words[g][:, k, :].bitcast(FP4X4),
+                    rhs_scale=d_scales[g][:, k, :],
                     start=(k == 0),
                     stop=False,
                 )
 
-        def mm_a(u):
-            t, g = place(u)
+        def matmul_a(unit):
+            t, g = place(unit)
             codes, scales = lhs["a", t, 0]
             for k in range(A_PASSES):
                 cols = slice(k * P, (k + 1) * P)
-                b_codes, b_scales = b_ops[g, k]
+                b_codes, b_scales = b_mx[g, k]
                 nc.tensor.matmul_mx(
-                    out=acc[u][:],
+                    out=acc[unit][:],
                     lhsT=codes[:, cols].bitcast(FP8X4),
                     lhsT_scale=scales[:, cols],
                     rhs=b_codes[:].bitcast(FP8X4),
@@ -224,242 +219,217 @@ def tile_half_squared_curve_factors_g5_kernel(
                     stop=(k == A_PASSES - 1),
                 )
 
-        def add(u):
-            t, g = place(u)
-            z[u] = work.tile([P, NT], F32, name="z", tag="z", bufs=6)
+        def add_carry(unit, lo=0, hi=CHUNK):
+            g = place(unit)[1]
+            if unit not in z:
+                z[unit] = work.tile([P, CHUNK], F32, name="z", bufs=7)
             nc.vector.scalar_tensor_tensor(
-                out=z[u][:], in0=acc[u][:], scalar=0.5, in1=carry_row[:, g * NT : (g + 1) * NT], op0=ALU.mult, op1=ALU.add
+                out=z[unit][:, lo:hi],
+                in0=acc[unit][:, lo:hi],
+                scalar=0.5,
+                in1=carry_row[:, g * CHUNK + lo : g * CHUNK + hi],
+                op0=ALU.mult,
+                op1=ALU.add,
             )
 
-        def square(u):
-            t, g = place(u)
-            y[u] = work.tile([P, NT], F32, name="y", tag="y", bufs=12)
-            nc.scalar.activation(out=y[u][:], in_=z[u][:], func=ACT.Square, scale=ROOT_TWO)
-            nc.sync.dma_start(out=out_0[t * P : (t + 1) * P, g * NT : (g + 1) * NT], in_=y[u][:])
+        def square(unit):
+            t, g = place(unit)
+            y[unit] = work.tile([P, CHUNK], F32, name="y", bufs=14)
+            nc.scalar.activation(out=y[unit][:], in_=z[unit][:], func=ACT.Square, scale=ROOT_TWO)
+            nc.sync.dma_start(out=out_0[t * P : (t + 1) * P, g * CHUNK : (g + 1) * CHUNK], in_=y[unit][:])
 
-        def cast(u):
-            y_sorted[u] = work.tile([P, NT], BF16, name="y_sorted", tag="y_sorted", bufs=10, align_bytes=64)
-            nc.vector.tensor_copy(
-                out=y_sorted[u][:].rearrange("s (u p e) -> s u p e", u=2, e=2),
-                in_=y[u][:].rearrange("s (p u e) -> s u p e", u=2, e=2),
-            )
+        def sorted_view(unit):
+            if unit not in y_sorted:
+                y_sorted[unit] = work.tile([P, CHUNK], BF16, name="y_sorted", bufs=10, align_bytes=64)
+            return y_sorted[unit][:].rearrange("s (u p e) -> s u p e", u=2, e=2)
 
-        def turn_out(pair):
-            bank = new_bank()
-            banks["y", pair] = bank
-            for j in range(2):
-                words = y_sorted[2 * pair + j][:].bitcast(F32)
-                for u in range(2):
-                    nc.tensor.transpose(bank[:, 2 * j + u, :], words[:, u * P : (u + 1) * P], ident[:])
+        def round_y(unit):
+            nc.vector.tensor_copy(out=sorted_view(unit), in_=y[unit][:].rearrange("s (p u e) -> s u p e", u=2, e=2))
 
-        early = 6 * P
-        y_scales = [
-            keep.tile([P, CHUNKS, early], U8, name="y_scales_early", align_bytes=64),
-            keep.tile([P, CHUNKS, S - early], U8, name="y_scales_late", align_bytes=64),
-        ]
-
-        def plane_of(g, m0, width):
-            if m0 < early:
-                return y_scales[0][:, g, m0 : m0 + width]
-            return y_scales[1][:, g, m0 - early : m0 - early + width]
-
-        def store_scales(part, queues):
-            words = slice(0, early // 4) if part == 0 else slice(early // 4, S // 4)
-            for q in range(4):
-                queues[q % len(queues)].dma_start(
-                    out=scales_hbm[:, 4 * q : 4 * q + 4, words].rearrange("g r w -> r g w"),
-                    in_=y_scales[part][32 * q : 32 * q + 4, :, :].bitcast(I32),
-                )
-
-        def quant_out(pair):
-            t, g = place(2 * pair)
-            codes = work.tile([P, 2 * P], U32, name="y_codes", tag="y_codes", bufs=4, align_bytes=64)
-            nc.vector.quantize_mx(out=codes[:].bitcast(FP8X4), scales=plane_of(g, t * P, 2 * P), in_=staged["y", pair][:])
-            nc.sync.dma_start(out=words_hbm[g, :, t * P : (t + 2) * P], in_=codes[:].bitcast(I32))
-            if pair == 8:
-                store_scales(0, [nc.sync])
-
-        def add_part(u, cols):
-            t, g = place(u)
-            nc.vector.scalar_tensor_tensor(
-                out=z[u][:, cols], in0=acc[u][:, cols], scalar=0.5, in1=carry_row[:, g * NT + cols.start : g * NT + cols.stop], op0=ALU.mult, op1=ALU.add
-            )
-
-        def square_sorted(u, h):
+        def square_rounded(unit, lo, hi):
             nc.scalar.activation(
-                out=y_sorted[u][:].rearrange("s (u p e) -> s u p e", u=2, e=2)[:, :, h * 64 : (h + 1) * 64, :],
-                in_=z[u][:, h * 256 : (h + 1) * 256].rearrange("s (p u e) -> s u p e", u=2, e=2),
+                out=sorted_view(unit)[:, :, lo // PACK : hi // PACK, :],
+                in_=z[unit][:, lo:hi].rearrange("s (p u e) -> s u p e", u=2, e=2),
                 func=ACT.Square,
                 scale=ROOT_TWO,
             )
 
-        def turn_one(u):
-            bank = new_bank()
-            banks["one", u] = bank
-            words = y_sorted[u][:].bitcast(F32)
-            for h in range(2):
-                nc.tensor.transpose(bank[:, h, :], words[:, h * P : (h + 1) * P], ident[:])
+        def turn_y(key, units):
+            duos = [y_sorted[unit][:].bitcast(F32) for unit in units]
+            turn(key, [words[:, u * P : (u + 1) * P] for words in duos for u in range(2)])
 
-        def copy_one(u, on_vector):
-            staged["one", u] = work.tile([P, KP], BF16, name="staged_one", tag="staged_one", bufs=2, align_bytes=64)
-            dst = staged["one", u][:].bitcast(F32).rearrange("p (s u) -> p s u", u=2)
-            src = banks["one", u][:, 0:2, :].rearrange("p u s -> p s u")
-            if on_vector:
-                nc.vector.tensor_copy(out=dst, in_=src)
-            else:
-                nc.scalar.copy(out=dst, in_=src)
+        def turn_pair(pair):
+            turn_y(("pair", pair), (2 * pair, 2 * pair + 1))
 
-        def quant_one(u, codes):
-            t, g = place(u)
+        def stage_unit(unit, copy):
+            staged["unit", unit] = work.tile([P, K_PASS], BF16, name="staged_unit", bufs=2, align_bytes=64)
+            interleave(("unit", unit), staged["unit", unit][:], 1, copy)
+
+        y_scales = [
+            keep.tile([P, CHUNKS, EARLY], U8, name="y_scales_early", align_bytes=64),
+            keep.tile([P, CHUNKS, S - EARLY], U8, name="y_scales_late", align_bytes=64),
+        ]
+
+        def quantise_y(key, unit, count):
+            t, g = place(unit)
+            pair, first = divmod(unit, 2)
+            if pair not in y_codes:
+                y_codes[pair] = work.tile([P, 2 * P], U32, name="y_codes", align_bytes=64)
+            part, m0 = (0, t * P) if t * P < EARLY else (1, t * P - EARLY)
             nc.vector.quantize_mx(
-                out=codes[:, (u % 2) * P : (u % 2 + 1) * P].bitcast(FP8X4),
-                scales=plane_of(g, t * P, P),
-                in_=staged["one", u][:],
+                out=y_codes[pair][:, first * P : (first + count) * P].bitcast(FP8X4),
+                scales=y_scales[part][:, g, m0 : m0 + count * P],
+                in_=staged[key][:],
             )
+            if first + count == 2:
+                cols = slice((t - first) * P, (t - first + 2) * P)
+                nc.sync.dma_start(out=y_words_hbm[g, :, cols], in_=y_codes[pair][:].bitcast(I32))
 
-        V, SC = True, False
-        turn_in("c", 0, 0)
-        presort("c", 0, 1, V)
-        turn_in("c", 0, 1)
-        copy_bank(("c", 0, 0))
-        copy_bank(("c", 0, 1), on_vector=True)
-        turn_carry(0)
-        turn_carry(1)
-        quant_in("c", 0, 0)
-        quant_in("c", 0, 1)
-        turn_in("c", 1, 0)
-        turn_in("c", 1, 1)
-        mm_c(0)
-        presort("c", 2, 0, V)
-        presort("c", 2, 1, V)
-        copy_carry(0)
-        copy_bank(("c", 1, 0))
-        copy_bank(("c", 1, 1))
-        copy_carry(1)
-        turn_in("c", 2, 0)
-        turn_in("c", 2, 1)
-        quant_in("c", 1, 0)
-        quant_in("c", 1, 1)
-        mm_c(1)
-        weave_b(0, 0, V)
-        copy_bank(("c", 2, 0))
-        copy_bank(("c", 2, 1))
-        weave_b(0, 1, V)
-        quant_in("c", 2, 0)
-        quant_in("c", 2, 1)
-        quant_b(0, 0)
-        quant_b(0, 1)
-        for t in (0, 1, 2):
-            turn_in("a", t, 0)
-        for t in (0, 1, 2):
-            copy_bank(("a", t, 0))
-        mm_c(2)
-        presort("c", 3, 0, V)
-        presort("c", 3, 1, V)
-        quant_in("a", 0, 0)
-        presort("a", 3, 0, V)
-        for t in (1, 2):
-            quant_in("a", t, 0)
-        third = (("c", 3, 0), ("c", 3, 1), ("a", 3, 0))
-        for key in third:
-            turn_in(*key)
-            copy_bank(key)
-        mm_a(0)
-        mm_a(1)
-        mm_a(2)
-        weave_b(1, 0, V, 0, 256)
-        quant_in(*third[0])
-        add(0)
-        quant_in(*third[1])
-        weave_b(1, 0, SC, 256, 512)
-        quant_in(*third[2])
-        add(1)
-        weave_b(1, 1, SC, 256, 512)
-        weave_b(1, 1, V, 0, 256)
-        mm_c(3)
-        mm_a(3)
-        mm_c(4)
-        add(2)
-        quant_b(1, 0)
-        quant_b(1, 1)
-        mm_c(5)
-        mm_a(4)
-        mm_a(5)
-        square(0)
-        square(1)
-        add(3)
-        square(2)
-        cast(0)
-        presort("c", 4, 0, V)
-        cast(1)
-        presort("c", 4, 1, V)
-        square(3)
-        add(4)
-        cast(2)
+        def quantise_pair(pair):
+            quantise_y(("pair", pair), 2 * pair, 2)
 
-        later = [(kind, t, half) for t in range(HALF_TILES, TILES) for kind, half in (("c", 0), ("c", 1), ("a", 0))]
-        for pair in range(3, 12):
-            keys = later[2 * (pair - 3) : 2 * (pair - 2)]
-            ahead = later[2 * (pair - 2) : 2 * (pair - 1)]
-            outs = [pair - 3] if pair < 9 else []
-            for key in keys:
-                turn_in(*key)
-            for o in outs:
-                turn_out(o)
+        def store_scales(part, queues):
+            words = slice(0, EARLY // 4) if part == 0 else slice(EARLY // 4, S // 4)
+            for q in range(4):
+                queues[q % len(queues)].dma_start(
+                    out=y_scales_hbm[:, 4 * q : 4 * q + 4, words].rearrange("g r w -> r g w"),
+                    in_=y_scales[part][32 * q : 32 * q + 4, :, :].bitcast(I32),
+                )
+
+        turn_strip(("c", 0, 0))
+        sort_strip(("c", 0, 1), on_vector)
+        turn_strip(("c", 0, 1))
+        stage(("c", 0, 0), on_scalar)
+        stage(("c", 0, 1), on_vector)
+        turn_carry(0, 2)
+        turn_carry(2, 1)
+        quantise_strip(("c", 0, 0))
+        quantise_strip(("c", 0, 1))
+        sort_strip(("c", 1, 1), on_scalar)
+        stage_carry(0, 2)
+        turn_strip(("c", 1, 0))
+        turn_strip(("c", 1, 1))
+        matmul_c(0)
+        for t in range(1, FIRST - 1):
+            for half in range(2):
+                sort_strip(("c", t + 1, half), on_vector)
+            for half in range(2):
+                stage(("c", t, half), on_scalar)
+            if t == 1:
+                stage_carry(2, 1)
+            for half in range(2):
+                turn_strip(("c", t + 1, half))
+            for half in range(2):
+                quantise_strip(("c", t, half))
+            matmul_c(t)
+        weave_b(0, 0, on_vector)
+        weave_b(0, 0, on_scalar)
+        for half in range(2):
+            stage(("c", FIRST - 1, half), on_scalar)
+        for t in range(2):
+            turn_strip(("a", t, 0))
+        for half in range(2):
+            quantise_strip(("c", FIRST - 1, half))
+        matmul_c(FIRST - 1)
+        stage(("a", 0, 0), on_scalar)
+        weave_b(0, 1, on_vector)
+        weave_b(0, 1, on_scalar)
+        stage(("a", 1, 0), on_scalar)
+        for k in range(A_PASSES):
+            quantise_b(0, k)
+            quantise_strip(("a", k, 0))
+        for t in range(2, FIRST):
+            turn_strip(("a", t, 0))
+            stage(("a", t, 0), on_scalar)
+            quantise_strip(("a", t, 0))
+        for unit in range(FIRST):
+            matmul_a(unit)
+
+        for k in range(A_PASSES):
+            weave_b(1, k, on_scalar)
+        for unit in range(FIRST):
+            add_carry(unit)
+            matmul_c(FIRST + unit)
+        for k in range(A_PASSES):
+            weave_b(1, k, on_vector)
+        for k in range(A_PASSES):
+            quantise_b(1, k)
+        for unit in range(FIRST):
+            matmul_a(FIRST + unit)
+            square(unit)
+        round_y(0)
+        round_y(1)
+        weave_b(2, 0, on_vector)
+        for k in range(A_PASSES):
+            weave_b(2, k, on_scalar)
+        for unit in range(FIRST, 2 * FIRST - 1):
+            add_carry(unit)
+        weave_b(2, 1, on_vector)
+        for k in range(A_PASSES):
+            quantise_b(2, k)
+            square(FIRST + k)
+        round_y(2)
+        round_y(3)
+
+        later = [(kind, t, half) for t in range(FIRST, TILES) for kind, half in (("c", 0), ("c", 1), ("a", 0))]
+        for pair in range(FIRST, PAIRS):
+            step = pair - FIRST
+            now = later[2 * step : 2 * step + 2]
+            ahead = later[2 * step + 2 : 2 * step + 4]
+            done = [pair - TURN_LAG] if now else []
+            rest = range(pair - TURN_LAG, pair - 1) if pair == PAIRS - 2 else []
+            for key in now:
+                turn_strip(key)
+            for old in done:
+                turn_pair(old)
             square(2 * pair - 2)
-            cast(2 * pair - 3)
-            add(2 * pair - 1)
+            round_y(2 * pair - 4)
+            add_carry(2 * pair - 1)
             for key in ahead[:1]:
-                presort(*key, on_vector=False)
-            for key in keys:
-                copy_bank(key)
-            for o in outs:
-                copy_bank(("y", o))
-            cast(2 * pair - 2)
+                sort_strip(key, on_scalar)
+            for key in now:
+                stage(key, on_scalar)
+            for old in done:
+                stage(("pair", old), on_scalar)
+            round_y(2 * pair - 3)
             for key in ahead[1:]:
-                presort(*key, on_vector=True)
-            if pair == 3:
-                weave_b(2, 0, V)
-                weave_b(2, 1, SC)
+                sort_strip(key, on_vector)
             square(2 * pair - 1)
-            for key in keys:
-                quant_in(*key)
-            mm_c(2 * pair)
-            mm_a(2 * pair)
-            if pair == 3:
-                quant_b(2, 0)
-            late = {10: [6, 7, 8], 11: [9]}.get(pair, [])
-            for o in late:
-                turn_out(o)
-            add(2 * pair)
-            for o in late:
-                copy_bank(("y", o))
-            if pair == 11:
-                cast(21)
-                square(22)
-            for o in outs + late:
-                quant_out(o)
-            if pair == 3:
-                quant_b(2, 1)
-            mm_c(2 * pair + 1)
-            mm_a(2 * pair + 1)
+            for key in now:
+                quantise_strip(key)
+            matmul_c(2 * pair)
+            matmul_a(2 * pair)
+            for old in rest:
+                turn_pair(old)
+            add_carry(2 * pair)
+            for old in rest:
+                stage(("pair", old), on_scalar)
+            for old in list(done) + list(rest):
+                quantise_pair(old)
+            if rest:
+                store_scales(0, [nc.sync])
+            matmul_c(2 * pair + 1)
+            matmul_a(2 * pair + 1)
 
-        cast(22)
-        turn_out(10)
-        turn_one(22)
-        z[23] = work.tile([P, NT], F32, name="z", tag="z", bufs=6)
-        y_sorted[23] = work.tile([P, NT], BF16, name="y_sorted", tag="y_sorted", bufs=10, align_bytes=64)
-        for h in range(2):
-            add_part(23, slice(h * 256, (h + 1) * 256))
-            square_sorted(23, h)
-        turn_one(23)
-        square(23)
-        copy_bank(("y", 10), V)
-        copy_one(22, V)
-        quant_out(10)
-        codes = work.tile([P, 2 * P], U32, name="y_codes", tag="y_codes", bufs=4, align_bytes=64)
-        quant_one(22, codes)
-        copy_one(23, V)
-        quant_one(23, codes)
-        nc.sync.dma_start(out=words_hbm[2, :, 6 * P : 8 * P], in_=codes[:].bitcast(I32))
+        last = UNITS - 1
+        round_y(last - 3)
+        round_y(last - 2)
+        square_rounded(last - 1, 0, CHUNK)
+        square(last - 1)
+        turn_pair(PAIRS - 3)
+        turn_pair(PAIRS - 2)
+        turn_y(("unit", last - 1), [last - 1])
+        for lo in (0, CHUNK // 2):
+            add_carry(last, lo, lo + CHUNK // 2)
+            square_rounded(last, lo, lo + CHUNK // 2)
+        turn_y(("unit", last), [last])
+        stage(("pair", PAIRS - 3), on_vector)
+        stage(("pair", PAIRS - 2), on_scalar)
+        stage_unit(last - 1, on_vector)
+        quantise_pair(PAIRS - 3)
+        quantise_y(("unit", last - 1), last - 1, 1)
+        quantise_pair(PAIRS - 2)
+        square(last)
+        stage_unit(last, on_scalar)
+        quantise_y(("unit", last), last, 1)
         store_scales(1, [nc.scalar, nc.sync])

import math
from contextlib import ExitStack

import concourse.mybir as mybir
from concourse.masks import make_identity

S, G, H, F = 1024, 1024, 2048, 1536
FLOPS = 2 * S * (G + H) * F

F32 = mybir.dt.float32
BF16 = mybir.dt.bfloat16
I32 = mybir.dt.int32
U32 = mybir.dt.uint32
U8 = mybir.dt.uint8
FP8X4 = mybir.dt.float8_e4m3fn_x4
FP4X4 = mybir.dt.float4_e2m1fn_x4
ACT = mybir.ActivationFunctionType
ALU = mybir.AluOpType

P = 128
PACK = 4
K_PASS = P * PACK
STRIP = 2 * K_PASS
CHUNK = 512
TILES = S // P
CHUNKS = F // CHUNK
A_PASSES = G // K_PASS
C_PASSES = H // K_PASS
UNITS = TILES * CHUNKS
PAIRS = UNITS // 2
FIRST = 4
EARLY = S - 2 * P
VECTOR_COLUMNS = (384, 192, 256)
TURN_LAG = 4
ROOT_TWO = math.sqrt(2.0)


def place(unit):
    if unit < CHUNKS * FIRST:
        return unit % FIRST, unit // FIRST
    couple, rest = divmod(unit - CHUNKS * FIRST, 2 * CHUNKS)
    return FIRST + 2 * couple + rest % 2, rest // 2


def tile_half_squared_curve_factors_g5_kernel(
    tc, govt_moves, govt_loadings, corp_moves, corp_words, corp_scales, carry, out_0, out_1, out_2
):
    nc = tc.nc
    on_vector = nc.vector.tensor_copy
    on_scalar = nc.scalar.copy
    with ExitStack() as ctx:
        keep = ctx.enter_context(tc.tile_pool(name="keep", bufs=1))
        work = ctx.enter_context(tc.tile_pool(name="work", bufs=4))
        psum = ctx.enter_context(tc.psum_pool(name="psum", bufs=4))
        ctx.enter_context(tc.manual_schedule())

        d_words_hbm = corp_words.bitcast(I32)
        d_scales_hbm = corp_scales.bitcast(I32)
        y_words_hbm = out_1.rearrange("g p m t -> g p (m t)").bitcast(I32)
        y_scales_hbm = out_2.bitcast(I32)

        strips, sorted_strips, banks, staged, lhs = {}, {}, {}, {}, {}
        d_words, b_rows, b_staged, b_mx = {}, {}, {}, {}
        acc, z, y, y_sorted, y_codes = {}, {}, {}, {}, {}

        ident = keep.tile([P, P], F32, name="ident", align_bytes=64)
        d_scales = [keep.tile([P, C_PASSES, CHUNK], U8, name="d_scales%d" % g, align_bytes=64) for g in range(CHUNKS)]
        carry_raw = keep.tile([P, CHUNKS, PACK], BF16, name="carry_raw")
        carry_half = keep.tile([P, CHUNKS * PACK], BF16, name="carry_half")
        for g in range(CHUNKS):
            nc.vector.memset(d_scales[g][:].rearrange("p k n -> p (k n)").bitcast(I32), 0)
        nc.gpsimd.dma_start(out=carry_raw[:], in_=carry.rearrange("(g p c) -> p g c", g=CHUNKS, c=PACK))
        make_identity(nc, ident[:])
        nc.scalar.activation(
            out=carry_half[:], in_=carry_raw[:].rearrange("p g c -> p (g c)"), func=ACT.Copy, scale=0.5
        )

        def load_rows(kind, t, width):
            src = corp_moves if kind == "c" else govt_moves
            for k0 in range(0, src.shape[1], width):
                rows = keep.tile([P, width], BF16, name="rows_%s%d_%d" % (kind, t, k0), align_bytes=64)
                nc.sync.dma_start(out=rows[:], in_=src[t * P : (t + 1) * P, k0 : k0 + width])
                for k in range(0, width, STRIP):
                    strips[kind, t, (k0 + k) // STRIP] = rows[:, k : k + STRIP]

        def load_d_words(g):
            d_words[g] = keep.tile([P, C_PASSES, 2 * CHUNK], U8, name="d_words%d" % g, align_bytes=64)
            cols = slice(g * CHUNK // 2, (g + 1) * CHUNK // 2)
            nc.sync.dma_start(
                out=d_words[g][:].bitcast(I32), in_=d_words_hbm[:, :, cols].rearrange("k p w -> p k w")
            )

        def load_d_scales(g):
            cols = slice(g * CHUNK // 4, (g + 1) * CHUNK // 4)
            for q in range(4):
                nc.sync.dma_start(
                    out=d_scales[g][32 * q : 32 * q + 4, :, :].bitcast(I32),
                    in_=d_scales_hbm[:, 4 * q : 4 * q + 4, cols].rearrange("k r w -> r k w"),
                )

        def load_b(g, k):
            b_rows[g, k] = keep.tile([P, PACK, CHUNK], BF16, name="b_rows%d_%d" % (g, k), align_bytes=64)
            rows = govt_loadings[k * K_PASS : (k + 1) * K_PASS, g * CHUNK : (g + 1) * CHUNK]
            nc.sync.dma_start(out=b_rows[g, k][:], in_=rows.rearrange("(p t) n -> p t n", t=PACK))

        load_rows("c", 0, STRIP)
        load_rows("c", 1, H)
        load_d_scales(0)
        load_d_words(0)
        for t in range(2, FIRST):
            load_rows("c", t, H)
        for k in range(A_PASSES):
            load_b(0, k)
            load_rows("a", 2 * k, G)
            load_rows("a", 2 * k + 1, G)
        load_d_words(1)
        load_d_scales(1)
        load_b(1, 0)
        load_b(1, 1)
        load_d_words(2)
        load_b(2, 0)
        load_rows("c", FIRST, H)
        load_b(2, 1)
        load_d_scales(2)
        load_rows("a", FIRST, G)
        for t in range(FIRST + 1, TILES):
            load_rows("c", t, H)
            load_rows("a", t, G)

        def sort_strip(key, copy):
            sorted_strips[key] = work.tile([P, 4, P], F32, name="sorted_strip", bufs=6, align_bytes=64)
            copy(
                out=sorted_strips[key][:].rearrange("s (j u) p -> s j u p", u=2),
                in_=strips[key].bitcast(F32).rearrange("s (j p u) -> s j u p", j=2, u=2),
            )

        def turn(key, sources):
            banks[key] = psum.tile([P, 4, P], F32, name="turned")
            for slot, source in enumerate(sources):
                nc.tensor.transpose(banks[key][:, slot, :], source, ident[:])

        def turn_strip(key):
            if key in sorted_strips:
                turn(key, [sorted_strips[key][:, slot, :] for slot in range(4)])
            else:
                duos = strips[key].bitcast(F32)
                turn(key, [duos[:, 2 * P * j + u : 2 * P * (j + 1) : 2] for j in range(2) for u in range(2)])

        def interleave(key, dst, count, copy):
            copy(
                out=dst.bitcast(F32).rearrange("p (j s u) -> p j s u", j=count, u=2),
                in_=banks[key][:, : 2 * count, :].rearrange("p (j u) s -> p j s u", u=2),
            )

        def stage(key, copy):
            staged[key] = work.tile([P, STRIP], BF16, name="staged", bufs=5, align_bytes=64)
            interleave(key, staged[key][:], 2, copy)

        def quantise_strip(key):
            codes = keep.tile([P, 2 * P], U32, name="lhs_codes_%s%d_%d" % key, align_bytes=64)
            scales = keep.tile([P, 2 * P], U8, name="lhs_scales_%s%d_%d" % key, align_bytes=64)
            lhs[key] = (codes, scales)
            nc.vector.quantize_mx(out=codes[:].bitcast(FP8X4), scales=scales[:], in_=staged[key][:])

        def weave_b(g, k, copy):
            if (g, k) not in b_staged:
                b_staged[g, k] = work.tile([P, CHUNK * PACK], BF16, name="b_staged", bufs=2, align_bytes=64)
            lo, hi = (0, VECTOR_COLUMNS[g]) if copy == on_vector else (VECTOR_COLUMNS[g], CHUNK)
            copy(
                out=b_staged[g, k][:, lo * PACK : hi * PACK].rearrange("p (c i t) -> p c t i", i=4, t=PACK),
                in_=b_rows[g, k][:, :, lo:hi].rearrange("p t (c i) -> p c t i", i=4),
            )

        def quantise_b(g, k):
            codes = keep.tile([P, CHUNK], U32, name="b_codes%d_%d" % (g, k), align_bytes=64)
            scales = keep.tile([P, CHUNK], U8, name="b_scales%d_%d" % (g, k), align_bytes=64)
            b_mx[g, k] = (codes, scales)
            nc.vector.quantize_mx(out=codes[:].bitcast(FP8X4), scales=scales[:], in_=b_staged[g, k][:])

        carry_row = keep.tile([P, F], BF16, name="carry_row", align_bytes=64)

        def turn_carry(g0, count):
            duos = carry_half[:].bitcast(F32)
            columns = range(2 * g0, 2 * (g0 + count))
            turn(("carry", g0), [duos[:, w : w + 1].to_broadcast([P, P]) for w in columns])

        def stage_carry(g0, count):
            interleave(("carry", g0), carry_row[:, g0 * CHUNK : (g0 + count) * CHUNK], count, on_scalar)

        def matmul_c(unit):
            t, g = place(unit)
            acc[unit] = psum.tile([P, CHUNK], F32, name="acc")
            for k in range(C_PASSES):
                codes, scales = lhs["c", t, k // 2]
                cols = slice((k % 2) * P, (k % 2 + 1) * P)
                nc.tensor.matmul_mx(
                    out=acc[unit][:],
                    lhsT=codes[:, cols].bitcast(FP8X4),
                    lhsT_scale=scales[:, cols],
                    rhs=d_words[g][:, k, :].bitcast(FP4X4),
                    rhs_scale=d_scales[g][:, k, :],
                    start=(k == 0),
                    stop=False,
                )

        def matmul_a(unit):
            t, g = place(unit)
            codes, scales = lhs["a", t, 0]
            for k in range(A_PASSES):
                cols = slice(k * P, (k + 1) * P)
                b_codes, b_scales = b_mx[g, k]
                nc.tensor.matmul_mx(
                    out=acc[unit][:],
                    lhsT=codes[:, cols].bitcast(FP8X4),
                    lhsT_scale=scales[:, cols],
                    rhs=b_codes[:].bitcast(FP8X4),
                    rhs_scale=b_scales[:],
                    start=False,
                    stop=(k == A_PASSES - 1),
                )

        def add_carry(unit, lo=0, hi=CHUNK):
            g = place(unit)[1]
            if unit not in z:
                z[unit] = work.tile([P, CHUNK], F32, name="z", bufs=7)
            nc.vector.scalar_tensor_tensor(
                out=z[unit][:, lo:hi],
                in0=acc[unit][:, lo:hi],
                scalar=0.5,
                in1=carry_row[:, g * CHUNK + lo : g * CHUNK + hi],
                op0=ALU.mult,
                op1=ALU.add,
            )

        def square(unit):
            t, g = place(unit)
            y[unit] = work.tile([P, CHUNK], F32, name="y", bufs=14)
            nc.scalar.activation(out=y[unit][:], in_=z[unit][:], func=ACT.Square, scale=ROOT_TWO)
            nc.sync.dma_start(out=out_0[t * P : (t + 1) * P, g * CHUNK : (g + 1) * CHUNK], in_=y[unit][:])

        def sorted_view(unit):
            if unit not in y_sorted:
                y_sorted[unit] = work.tile([P, CHUNK], BF16, name="y_sorted", bufs=10, align_bytes=64)
            return y_sorted[unit][:].rearrange("s (u p e) -> s u p e", u=2, e=2)

        def round_y(unit):
            nc.vector.tensor_copy(out=sorted_view(unit), in_=y[unit][:].rearrange("s (p u e) -> s u p e", u=2, e=2))

        def square_rounded(unit, lo, hi):
            nc.scalar.activation(
                out=sorted_view(unit)[:, :, lo // PACK : hi // PACK, :],
                in_=z[unit][:, lo:hi].rearrange("s (p u e) -> s u p e", u=2, e=2),
                func=ACT.Square,
                scale=ROOT_TWO,
            )

        def turn_y(key, units):
            duos = [y_sorted[unit][:].bitcast(F32) for unit in units]
            turn(key, [words[:, u * P : (u + 1) * P] for words in duos for u in range(2)])

        def turn_pair(pair):
            turn_y(("pair", pair), (2 * pair, 2 * pair + 1))

        def stage_unit(unit, copy):
            staged["unit", unit] = work.tile([P, K_PASS], BF16, name="staged_unit", bufs=2, align_bytes=64)
            interleave(("unit", unit), staged["unit", unit][:], 1, copy)

        y_scales = [
            keep.tile([P, CHUNKS, EARLY], U8, name="y_scales_early", align_bytes=64),
            keep.tile([P, CHUNKS, S - EARLY], U8, name="y_scales_late", align_bytes=64),
        ]

        def quantise_y(key, unit, count):
            t, g = place(unit)
            pair, first = divmod(unit, 2)
            if pair not in y_codes:
                y_codes[pair] = work.tile([P, 2 * P], U32, name="y_codes", align_bytes=64)
            part, m0 = (0, t * P) if t * P < EARLY else (1, t * P - EARLY)
            nc.vector.quantize_mx(
                out=y_codes[pair][:, first * P : (first + count) * P].bitcast(FP8X4),
                scales=y_scales[part][:, g, m0 : m0 + count * P],
                in_=staged[key][:],
            )
            if first + count == 2:
                cols = slice((t - first) * P, (t - first + 2) * P)
                nc.sync.dma_start(out=y_words_hbm[g, :, cols], in_=y_codes[pair][:].bitcast(I32))

        def quantise_pair(pair):
            quantise_y(("pair", pair), 2 * pair, 2)

        def store_scales(part, queues):
            words = slice(0, EARLY // 4) if part == 0 else slice(EARLY // 4, S // 4)
            for q in range(4):
                queues[q % len(queues)].dma_start(
                    out=y_scales_hbm[:, 4 * q : 4 * q + 4, words].rearrange("g r w -> r g w"),
                    in_=y_scales[part][32 * q : 32 * q + 4, :, :].bitcast(I32),
                )

        turn_strip(("c", 0, 0))
        sort_strip(("c", 0, 1), on_vector)
        turn_strip(("c", 0, 1))
        stage(("c", 0, 0), on_scalar)
        stage(("c", 0, 1), on_vector)
        turn_carry(0, 2)
        turn_carry(2, 1)
        quantise_strip(("c", 0, 0))
        quantise_strip(("c", 0, 1))
        sort_strip(("c", 1, 1), on_scalar)
        stage_carry(0, 2)
        turn_strip(("c", 1, 0))
        turn_strip(("c", 1, 1))
        matmul_c(0)
        for t in range(1, FIRST - 1):
            for half in range(2):
                sort_strip(("c", t + 1, half), on_vector)
            for half in range(2):
                stage(("c", t, half), on_scalar)
            if t == 1:
                stage_carry(2, 1)
            for half in range(2):
                turn_strip(("c", t + 1, half))
            for half in range(2):
                quantise_strip(("c", t, half))
            matmul_c(t)
        weave_b(0, 0, on_vector)
        weave_b(0, 0, on_scalar)
        for half in range(2):
            stage(("c", FIRST - 1, half), on_scalar)
        for t in range(2):
            turn_strip(("a", t, 0))
        for half in range(2):
            quantise_strip(("c", FIRST - 1, half))
        matmul_c(FIRST - 1)
        stage(("a", 0, 0), on_scalar)
        weave_b(0, 1, on_vector)
        weave_b(0, 1, on_scalar)
        stage(("a", 1, 0), on_scalar)
        for k in range(A_PASSES):
            quantise_b(0, k)
            quantise_strip(("a", k, 0))
        for t in range(2, FIRST):
            turn_strip(("a", t, 0))
            stage(("a", t, 0), on_scalar)
            quantise_strip(("a", t, 0))
        for unit in range(FIRST):
            matmul_a(unit)

        for k in range(A_PASSES):
            weave_b(1, k, on_scalar)
        for unit in range(FIRST):
            add_carry(unit)
            matmul_c(FIRST + unit)
        for k in range(A_PASSES):
            weave_b(1, k, on_vector)
        for k in range(A_PASSES):
            quantise_b(1, k)
        for unit in range(FIRST):
            matmul_a(FIRST + unit)
            square(unit)
        round_y(0)
        round_y(1)
        weave_b(2, 0, on_vector)
        for k in range(A_PASSES):
            weave_b(2, k, on_scalar)
        for unit in range(FIRST, 2 * FIRST - 1):
            add_carry(unit)
        weave_b(2, 1, on_vector)
        for k in range(A_PASSES):
            quantise_b(2, k)
            square(FIRST + k)
        round_y(2)
        round_y(3)

        later = [(kind, t, half) for t in range(FIRST, TILES) for kind, half in (("c", 0), ("c", 1), ("a", 0))]
        for pair in range(FIRST, PAIRS):
            step = pair - FIRST
            now = later[2 * step : 2 * step + 2]
            ahead = later[2 * step + 2 : 2 * step + 4]
            done = [pair - TURN_LAG] if now else []
            rest = range(pair - TURN_LAG, pair - 1) if pair == PAIRS - 2 else []
            for key in now:
                turn_strip(key)
            for old in done:
                turn_pair(old)
            square(2 * pair - 2)
            round_y(2 * pair - 4)
            add_carry(2 * pair - 1)
            for key in ahead[:1]:
                sort_strip(key, on_scalar)
            for key in now:
                stage(key, on_scalar)
            for old in done:
                stage(("pair", old), on_scalar)
            round_y(2 * pair - 3)
            for key in ahead[1:]:
                sort_strip(key, on_vector)
            square(2 * pair - 1)
            for key in now:
                quantise_strip(key)
            matmul_c(2 * pair)
            matmul_a(2 * pair)
            for old in rest:
                turn_pair(old)
            add_carry(2 * pair)
            for old in rest:
                stage(("pair", old), on_scalar)
            for old in list(done) + list(rest):
                quantise_pair(old)
            if rest:
                store_scales(0, [nc.sync])
            matmul_c(2 * pair + 1)
            matmul_a(2 * pair + 1)

        last = UNITS - 1
        round_y(last - 3)
        round_y(last - 2)
        square_rounded(last - 1, 0, CHUNK)
        square(last - 1)
        turn_pair(PAIRS - 3)
        turn_pair(PAIRS - 2)
        turn_y(("unit", last - 1), [last - 1])
        for lo in (0, CHUNK // 2):
            add_carry(last, lo, lo + CHUNK // 2)
            square_rounded(last, lo, lo + CHUNK // 2)
        turn_y(("unit", last), [last])
        stage(("pair", PAIRS - 3), on_vector)
        stage(("pair", PAIRS - 2), on_scalar)
        stage_unit(last - 1, on_vector)
        quantise_pair(PAIRS - 3)
        quantise_y(("unit", last - 1), last - 1, 1)
        quantise_pair(PAIRS - 2)
        square(last)
        stage_unit(last, on_scalar)
        quantise_y(("unit", last), last, 1)
        store_scales(1, [nc.scalar, nc.sync])
